import numpy as np
import ml_dtypes


def mxq(x, axis, fmt="e4m3"):
    dtype, down = {"e4m3": (ml_dtypes.float8_e4m3fn, 7), "e5m2": (ml_dtypes.float8_e5m2, 14)}[fmt]
    v = np.moveaxis(np.asarray(x, np.float32).astype(ml_dtypes.bfloat16).astype(np.float64), axis, -1)
    blocks = v.reshape(v.shape[:-1] + (-1, 32))
    amax = np.abs(blocks).max(-1, keepdims=True)
    byte = np.maximum(np.where(amax > 0, np.frexp(amax)[1] - 1 + 127, 0) - down, 1)
    scale = np.exp2(byte - 127.0)
    codes = (blocks / scale).astype(np.float32).astype(dtype).astype(np.float64)
    return np.moveaxis((codes * scale).reshape(v.shape), -1, axis)


WIDE = False


def mx_kscale(k):
    if not WIDE:
        return np.ones(k)
    levels = np.array([10, -10, 5, -5, 0])
    if k % 512:
        return np.exp2(np.random.permutation(np.resize(levels, k // 32))).repeat(32)
    a = np.empty((k // 512, 16))
    for p in range(k // 512):
        a[p, :8] = np.random.permutation(np.resize(levels, 8))
        for g in range(8):
            far = levels[np.abs(levels - a[p, g]) >= 10]
            a[p, g + 8] = far[np.random.randint(len(far))]
    return np.exp2(a.ravel()).repeat(32)


def f64(x):
    return np.asarray(x).astype(np.float64)


def striped(idx):
    return np.tile(idx.reshape(-1, 16).T, (8, 1)).astype(np.uint16)


def unstriped(offs):
    return offs[:16].T.reshape(-1).astype(np.int64)


def pack_weight(w):
    k, n = w.shape
    w = f64(np.asarray(w, np.float32).astype(ml_dtypes.bfloat16)).reshape(k // 32, 32, n)
    amax = np.abs(w).max(1)
    byte = np.clip(np.where(amax > 0, np.frexp(amax)[1] - 1 + 127 - 7, 1), 1, 254)
    scaled = (w * np.exp2(127.0 - byte)[:, None, :]).reshape(k, n).astype(np.float32)
    words = np.ascontiguousarray(scaled.reshape(k // 512, 128, 4, n).transpose(0, 1, 3, 2)).astype(ml_dtypes.float8_e4m3fn).view(np.uint8)
    return words, np.ascontiguousarray(byte.astype(np.uint8).reshape(k // 512, 16, n))


def unpack_weight(words, scales):
    g, p, n, _ = words.shape
    vals = np.ascontiguousarray(words).view(ml_dtypes.float8_e4m3fn).astype(np.float64) * np.repeat(np.exp2(scales.astype(np.float64) - 127.0), 8, axis=1)[..., None]
    return vals.transpose(0, 1, 3, 2).reshape(g * 512, n)


def silu(v):
    return v / (1.0 + np.exp(-np.maximum(v, -700.0)))


K, T, S, D, N, H, V, U = 1024, 2048, 512, 2, 128, 512, 256, 512


def setup_inputs():
    n = np.random.standard_normal
    s = mx_kscale(K)[:, None]
    u = mx_kscale(H)
    packed_xT = pack_weight(n((K, T)) * s)
    return {
        "x_words": packed_xT[0],
        "x_scales": packed_xT[1],
        "hT": (n((K, H)) / np.sqrt(K) / s).astype(np.float32),
        "own": (0.7 * n((H, U))).astype(np.float32),
        "unit": (np.random.uniform(0.6, 1.4, (H, 1)) * u[:, None]).astype(np.float32),
        "w1": (n((H, N)) / np.sqrt(H) / u[:, None]).astype(np.float32),
        "offs": striped(np.random.permutation(T)[:S]),
        "ven": striped(np.random.permutation(np.concatenate([np.arange(V), np.random.randint(0, V, U - V)]))),
        "coc": striped(np.random.permutation(U)),
    }


def reference(x_words, x_scales, hT, own, unit, w1, offs, ven, coc):
    hTq = mxq(f64(hT), 0, "e4m3")
    xq = unpack_weight(x_words, x_scales)[:, unstriped(offs)]
    y = hTq.T @ xq
    aff = np.tanh(y)
    venue = aff.reshape(len(aff), -1, D).max(axis=2)
    vv = venue[:, unstriped(ven)]
    hv = vv + f64(own)
    hid = f64(unit) * (silu(hv) + hv[:, unstriped(coc)])
    return mxq(f64(w1), 0, "e4m3").T @ mxq(hid, 0, "e4m3")

@@ -1,0 +1,254 @@
+from contextlib import ExitStack
+
+import concourse.mybir as mybir
+
+K, T, S, H, V, N = 1024, 2048, 512, 512, 256, 128
+FLOPS = 2 * K * H * S + 2 * H * N * S
+
+F32 = mybir.dt.float32
+BF16 = mybir.dt.bfloat16
+I32 = mybir.dt.int32
+U32 = mybir.dt.uint32
+U16 = mybir.dt.uint16
+U8 = mybir.dt.uint8
+FP8X4 = mybir.dt.float8_e4m3fn_x4
+ACT = mybir.ActivationFunctionType
+ALU = mybir.AluOpType
+
+P = 128
+PACK = 4
+PASSES = K // (P * PACK)
+HALF = S // 2
+SCALAR_VEN = (2, 3)
+
+
+def tile_picked_yhlgnn_silu_p_kernel(
+    tc, x_words, x_scales, hT, own, unit, w1, offs, ven, coc, out
+):
+    nc = tc.nc
+    with ExitStack() as ctx:
+        lists = ctx.enter_context(tc.tile_pool(name="lists", bufs=1))
+        sb = ctx.enter_context(tc.tile_pool(name="sb", bufs=1))
+        ps = ctx.enter_context(tc.psum_pool(name="ps", bufs=1))
+
+        offs_sb = lists.tile([P, S // 16], U16, name="offs_sb")
+        ven_sb = lists.tile([P, S // 16], U16, name="ven_sb")
+        coc_sb = lists.tile([P, S // 16], U16, name="coc_sb")
+
+        xs_all = sb.tile([P, T], U8, name="xs_all", align_bytes=64)
+        nc.vector.memset(xs_all[:].bitcast(I32), 0)
+        for q in range(4):
+            nc.scalar.dma_start(
+                out=xs_all[32 * q : 32 * q + 8, :].bitcast(I32),
+                in_=x_scales[:, 4 * q : 4 * q + 4, :].bitcast(I32),
+            )
+
+        h_raw = [sb.tile([P, PACK, H], F32, name=f"h_raw{o}") for o in range(PASSES)]
+        xw_all = [sb.tile([P, T], I32, name=f"xw_all{o}") for o in range(PASSES)]
+        own_sb = [sb.tile([P, S], F32, name=f"own_sb{t}") for t in range(PACK)]
+        unit_sb = sb.tile([P, PACK], F32, name="unit_sb")
+        w_raw = sb.tile([P, PACK, N], F32, name="w_raw")
+
+        def load_h(o):
+            nc.sync.dma_start(
+                out=h_raw[o][:],
+                in_=hT[512 * o : 512 * (o + 1), :].rearrange("(p j) c -> p j c", j=PACK),
+            )
+
+        load_h(0)
+        nc.sync.dma_start(offs_sb[:], offs)
+        nc.sync.dma_start(ven_sb[:], ven)
+        nc.sync.dma_start(coc_sb[:], coc)
+        nc.sync.dma_start(out=unit_sb[:], in_=unit.rearrange("(p t) o -> p (t o)", t=PACK))
+        load_h(1)
+        for o in range(PASSES):
+            nc.sync.dma_start(
+                out=xw_all[o][:],
+                in_=x_words[o].rearrange("p n t -> p (n t)").bitcast(I32),
+            )
+        own_rows = own.rearrange("(p t) j -> p t j", t=PACK)
+        for t in range(PACK):
+            nc.sync.dma_start(out=own_sb[t][:], in_=own_rows[:, t, :])
+        nc.sync.dma_start(out=w_raw[:], in_=w1.rearrange("(p j) m -> p j m", j=PACK))
+
+        h_codes = [sb.tile([P, H], U32, name=f"h_codes{o}", align_bytes=64) for o in range(PASSES)]
+        h_scales = [sb.tile([P, H], U8, name=f"h_scales{o}", align_bytes=64) for o in range(PASSES)]
+        h_bf = {}
+
+        def round_h(o, u):
+            h_bf[o, u] = sb.tile([P, 2, P, PACK], BF16, name=f"h_bf{o}{u}", align_bytes=64)
+            src = h_raw[o][:].rearrange("p j (m t) -> p m j t", t=PACK)[:, :, :, 2 * u : 2 * u + 2]
+            dst = h_bf[o, u][:].rearrange("p t m j -> p m j t")
+            if u == 0:
+                nc.vector.tensor_copy(out=dst, in_=src)
+            else:
+                nc.scalar.copy(out=dst, in_=src)
+
+        def quantize_h(o, u):
+            cols = slice(2 * P * u, 2 * P * (u + 1))
+            nc.vector.quantize_mx(
+                out=h_codes[o][:, cols].bitcast(FP8X4),
+                scales=h_scales[o][:, cols],
+                in_=h_bf[o, u][:].rearrange("p t m j -> p (t m j)"),
+            )
+
+        x_codes = [sb.tile([P, S], U32, name=f"x_codes{o}", align_bytes=64) for o in range(PASSES)]
+        x_planes = sb.tile([P, S], U8, name="x_planes", align_bytes=64)
+
+        def gather_words(o):
+            nc.vector.tensor_copy(x_codes[o][:], xw_all[o][:].bitcast(U32).indirect(offs_sb[:]))
+
+        y = [ps.tile([P, S], F32, name=f"y{t}") for t in range(PACK)]
+
+        def first_product(o):
+            for t in range(PACK):
+                cols = slice(P * t, P * (t + 1))
+                nc.tensor.matmul_mx(
+                    out=y[t][:],
+                    lhsT=h_codes[o][:, cols].bitcast(FP8X4),
+                    lhsT_scale=h_scales[o][:, cols],
+                    rhs=x_codes[o][:].bitcast(FP8X4),
+                    rhs_scale=x_planes[4 * o : P, :],
+                    start=(o == 0),
+                    stop=(o == PASSES - 1),
+                )
+
+        round_h(0, 0)
+        round_h(0, 1)
+        nc.vector.tensor_copy(x_planes[:], xs_all[:].indirect(offs_sb[:]))
+        quantize_h(0, 0)
+        quantize_h(0, 1)
+        round_h(1, 0)
+        round_h(1, 1)
+        quantize_h(1, 0)
+        quantize_h(1, 1)
+        gather_words(0)
+        first_product(0)
+        gather_words(1)
+        first_product(1)
+
+        va = [sb.tile([P, V + S], F32, name=f"va{t}") for t in range(PACK)]
+        hv = [sb.tile([P, S], F32, name=f"hv{t}") for t in range(PACK)]
+        vv = {t: sb.tile([P, S], F32, name=f"vv{t}") for t in SCALAR_VEN}
+        act = [sb.tile([P, S], F32, name=f"act{t}") for t in range(PACK)]
+        g = [[sb.tile([P, HALF], F32, name=f"g{t}{u}") for u in range(2)] for t in range(PACK)]
+
+        def bound(t):
+            nc.scalar.activation(va[t][:, V:], y[t][:], ACT.Tanh)
+
+        def pair_max(t):
+            nc.vector.tensor_tensor(va[t][:, :V], va[t][:, V::2], va[t][:, V + 1 :: 2], ALU.max)
+
+        def look_up(t):
+            if t in SCALAR_VEN:
+                nc.scalar.activation(vv[t][:], va[t][:].indirect(ven_sb[:]), ACT.Copy)
+            else:
+                nc.vector.tensor_tensor(hv[t][:], va[t][:].indirect(ven_sb[:]), own_sb[t][:], ALU.add)
+
+        def add_own(t):
+            if t in SCALAR_VEN:
+                nc.vector.tensor_tensor(hv[t][:], vv[t][:], own_sb[t][:], ALU.add)
+
+        def silu(t):
+            nc.scalar.activation(act[t][:], hv[t][:], ACT.Silu)
+
+        def join(t, u):
+            nc.vector.tensor_tensor(
+                g[t][u][:],
+                hv[t][:].indirect(coc_sb[:, 16 * u : 16 * (u + 1)]),
+                act[t][:, HALF * u : HALF * (u + 1)],
+                ALU.add,
+            )
+
+        hid_planes = [sb.tile([P, PACK, HALF], BF16, name=f"hid_planes{u}", align_bytes=64) for u in range(2)]
+
+        def scale(t, u):
+            nc.scalar.activation(hid_planes[u][:, t, :], g[t][u][:], ACT.Copy, scale=unit_sb[:, t : t + 1])
+
+        w_bf = sb.tile([P, N, PACK], BF16, name="w_bf", align_bytes=64)
+        w_codes = sb.tile([P, N], U32, name="w_codes", align_bytes=64)
+        w_scales = sb.tile([P, N], U8, name="w_scales", align_bytes=64)
+
+        def round_w():
+            nc.vector.tensor_copy(
+                out=w_bf[:].rearrange("p (c i) j -> p c j i", i=4),
+                in_=w_raw[:].rearrange("p j (c i) -> p c j i", i=4),
+            )
+
+        def quantize_w():
+            nc.vector.quantize_mx(
+                out=w_codes[:].bitcast(FP8X4),
+                scales=w_scales[:],
+                in_=w_bf[:].rearrange("p m j -> p (m j)"),
+            )
+
+        hid_bf = [sb.tile([P, HALF, PACK], BF16, name=f"hid_bf{u}", align_bytes=64) for u in range(2)]
+        hid_codes = [sb.tile([P, HALF], U32, name=f"hid_codes{u}", align_bytes=64) for u in range(2)]
+        hid_scales = [sb.tile([P, HALF], U8, name=f"hid_scales{u}", align_bytes=64) for u in range(2)]
+
+        def interleave(u):
+            nc.vector.tensor_copy(
+                out=hid_bf[u][:].rearrange("p (c i) t -> p c t i", i=4),
+                in_=hid_planes[u][:].rearrange("p t (c i) -> p c t i", i=4),
+            )
+
+        def finish(u):
+            nc.vector.quantize_mx(
+                out=hid_codes[u][:].bitcast(FP8X4),
+                scales=hid_scales[u][:],
+                in_=hid_bf[u][:].rearrange("p c t -> p (c t)"),
+            )
+            acc = ps.tile([P, HALF], F32, name=f"acc{u}")
+            nc.tensor.matmul_mx(
+                out=acc[:],
+                lhsT=w_codes[:].bitcast(FP8X4),
+                lhsT_scale=w_scales[:],
+                rhs=hid_codes[u][:].bitcast(FP8X4),
+                rhs_scale=hid_scales[u][:],
+                start=True,
+                stop=True,
+            )
+            res = sb.tile([P, HALF], F32, name=f"res{u}")
+            nc.scalar.copy(out=res[:], in_=acc[:])
+            nc.sync.dma_start(out=out[:, HALF * u : HALF * (u + 1)], in_=res[:])
+
+        bound(0)
+        pair_max(0)
+        bound(1)
+        pair_max(1)
+        look_up(0)
+        bound(2)
+        pair_max(2)
+        bound(3)
+        pair_max(3)
+        look_up(1)
+        silu(0)
+        look_up(2)
+        round_w()
+        join(0, 0)
+        silu(1)
+        look_up(3)
+        quantize_w()
+        add_own(2)
+        join(1, 0)
+        silu(2)
+        add_own(3)
+        join(0, 1)
+        silu(3)
+        join(2, 0)
+        scale(0, 0)
+        scale(1, 0)
+        join(3, 0)
+        scale(2, 0)
+        join(1, 1)
+        scale(3, 0)
+        join(2, 1)
+        scale(0, 1)
+        scale(1, 1)
+        join(3, 1)
+        scale(2, 1)
+        interleave(0)
+        scale(3, 1)
+        finish(0)
+        interleave(1)
+        finish(1)

@@ -19,7 +19,10 @@ P = 128
 PACK = 4
 PASSES = K // (P * PACK)
 HALF = S // 2
-SCALAR_VEN = (2, 3)
+VECTOR_MAX = (1,)
+PIECES = ((0, 256), (256, 384), (384, 512))
+LAST = len(PIECES) - 1
+SCALAR_VEN = (1, 2, 3)
 
 
 def tile_picked_yhlgnn_silu_p_kernel(
@@ -44,10 +47,24 @@ def tile_picked_yhlgnn_silu_p_kernel(
             )
 
         h_raw = [sb.tile([P, PACK, H], F32, name=f"h_raw{o}") for o in range(PASSES)]
-        xw_all = [sb.tile([P, T], I32, name=f"xw_all{o}") for o in range(PASSES)]
+        xw_all = [sb.tile([P, T], I32, name=f"xw_all{o}", tag=f"words{o}", align_bytes=64) for o in range(PASSES)]
         own_sb = [sb.tile([P, S], F32, name=f"own_sb{t}") for t in range(PACK)]
         unit_sb = sb.tile([P, PACK], F32, name="unit_sb")
         w_raw = sb.tile([P, PACK, N], F32, name="w_raw")
+
+        own_rows = own.rearrange("(p t) j -> p t j", t=PACK)
+
+        def load_x(o):
+            nc.sync.dma_start(
+                out=xw_all[o][:],
+                in_=x_words[o].rearrange("p n t -> p (n t)").bitcast(I32),
+            )
+
+        def load_w():
+            nc.sync.dma_start(out=w_raw[:], in_=w1.rearrange("(p j) m -> p j m", j=PACK))
+
+        def load_own(t):
+            nc.sync.dma_start(out=own_sb[t][:], in_=own_rows[:, t, :])
 
         def load_h(o):
             nc.sync.dma_start(
@@ -56,20 +73,23 @@ def tile_picked_yhlgnn_silu_p_kernel(
             )
 
         load_h(0)
+        load_h(1)
         nc.sync.dma_start(offs_sb[:], offs)
         nc.sync.dma_start(ven_sb[:], ven)
+        load_x(0)
+        load_x(1)
+        load_w()
+        load_own(0)
+        load_own(1)
         nc.sync.dma_start(coc_sb[:], coc)
+        load_own(2)
+        load_own(3)
         nc.sync.dma_start(out=unit_sb[:], in_=unit.rearrange("(p t) o -> p (t o)", t=PACK))
-        load_h(1)
-        for o in range(PASSES):
-            nc.sync.dma_start(
-                out=xw_all[o][:],
-                in_=x_words[o].rearrange("p n t -> p (n t)").bitcast(I32),
-            )
-        own_rows = own.rearrange("(p t) j -> p t j", t=PACK)
-        for t in range(PACK):
-            nc.sync.dma_start(out=own_sb[t][:], in_=own_rows[:, t, :])
-        nc.sync.dma_start(out=w_raw[:], in_=w1.rearrange("(p j) m -> p j m", j=PACK))
+
+        warm = sb.tile([P, 1], F32, name="warm")
+        nc.vector.memset(warm[:], 0.0)
+        warm_out = sb.tile([P, 1], F32, name="warm_out")
+        nc.scalar.activation(warm_out[:], warm[:], ACT.Silu)
 
         h_codes = [sb.tile([P, H], U32, name=f"h_codes{o}", align_bytes=64) for o in range(PASSES)]
         h_scales = [sb.tile([P, H], U8, name=f"h_scales{o}", align_bytes=64) for o in range(PASSES)]
@@ -77,8 +97,8 @@ def tile_picked_yhlgnn_silu_p_kernel(
 
         def round_h(o, u):
             h_bf[o, u] = sb.tile([P, 2, P, PACK], BF16, name=f"h_bf{o}{u}", align_bytes=64)
-            src = h_raw[o][:].rearrange("p j (m t) -> p m j t", t=PACK)[:, :, :, 2 * u : 2 * u + 2]
-            dst = h_bf[o, u][:].rearrange("p t m j -> p m j t")
+            src = h_raw[o][:].rearrange("p j (m t) -> p m t j", t=PACK)[:, :, 2 * u : 2 * u + 2, :]
+            dst = h_bf[o, u][:].rearrange("p t m j -> p m t j")
             if u == 0:
                 nc.vector.tensor_copy(out=dst, in_=src)
             else:
@@ -92,58 +112,68 @@ def tile_picked_yhlgnn_silu_p_kernel(
                 in_=h_bf[o, u][:].rearrange("p t m j -> p (t m j)"),
             )
 
-        x_codes = [sb.tile([P, S], U32, name=f"x_codes{o}", align_bytes=64) for o in range(PASSES)]
         x_planes = sb.tile([P, S], U8, name="x_planes", align_bytes=64)
-
-        def gather_words(o):
-            nc.vector.tensor_copy(x_codes[o][:], xw_all[o][:].bitcast(U32).indirect(offs_sb[:]))
-
         y = [ps.tile([P, S], F32, name=f"y{t}") for t in range(PACK)]
 
-        def first_product(o):
+        def first_product(o, u):
+            half = slice(HALF * u, HALF * (u + 1))
+            x_codes = sb.tile([P, HALF], U32, name=f"x_codes{o}{u}", align_bytes=64)
+            nc.vector.tensor_copy(x_codes[:], xw_all[o][:].bitcast(U32).indirect(offs_sb[:, 16 * u : 16 * (u + 1)]))
             for t in range(PACK):
                 cols = slice(P * t, P * (t + 1))
                 nc.tensor.matmul_mx(
-                    out=y[t][:],
+                    out=y[t][:, half],
                     lhsT=h_codes[o][:, cols].bitcast(FP8X4),
                     lhsT_scale=h_scales[o][:, cols],
-                    rhs=x_codes[o][:].bitcast(FP8X4),
-                    rhs_scale=x_planes[4 * o : P, :],
-                    start=(o == 0),
-                    stop=(o == PASSES - 1),
+                    rhs=x_codes[:].bitcast(FP8X4),
+                    rhs_scale=x_planes[4 * o : P, half],
+                    start=(o == 0 and u == 0),
+                    stop=(o == PASSES - 1 and u == 1),
                 )
 
         round_h(0, 0)
         round_h(0, 1)
-        nc.vector.tensor_copy(x_planes[:], xs_all[:].indirect(offs_sb[:]))
         quantize_h(0, 0)
         quantize_h(0, 1)
         round_h(1, 0)
         round_h(1, 1)
         quantize_h(1, 0)
         quantize_h(1, 1)
-        gather_words(0)
-        first_product(0)
-        gather_words(1)
-        first_product(1)
+        nc.vector.tensor_copy(x_planes[:], xs_all[:].indirect(offs_sb[:]))
+        for o in range(PASSES):
+            for u in range(2):
+                first_product(o, u)
 
-        va = [sb.tile([P, V + S], F32, name=f"va{t}") for t in range(PACK)]
+        va = [sb.tile([P, V + (V if t in VECTOR_MAX else S)], F32, name=f"va{t}") for t in range(PACK)]
         hv = [sb.tile([P, S], F32, name=f"hv{t}") for t in range(PACK)]
         vv = {t: sb.tile([P, S], F32, name=f"vv{t}") for t in SCALAR_VEN}
         act = [sb.tile([P, S], F32, name=f"act{t}") for t in range(PACK)]
-        g = [[sb.tile([P, HALF], F32, name=f"g{t}{u}") for u in range(2)] for t in range(PACK)]
+        g = [[sb.tile([P, b - a], F32, name=f"g{t}{u}") for u, (a, b) in enumerate(PIECES)] for t in range(PACK)]
 
-        def bound(t):
-            nc.scalar.activation(va[t][:, V:], y[t][:], ACT.Tanh)
+        def empty_bank(t):
+            if t in VECTOR_MAX:
+                nc.vector.tensor_reduce(
+                    va[t][:, V:], y[t][:].rearrange("p (v d) -> p v d", d=2), mybir.AxisListType.X, ALU.max
+                )
+            else:
+                nc.scalar.activation(va[t][:, V:], y[t][:], ACT.Tanh)
 
-        def pair_max(t):
-            nc.vector.tensor_tensor(va[t][:, :V], va[t][:, V::2], va[t][:, V + 1 :: 2], ALU.max)
+        def venue(t):
+            if t in VECTOR_MAX:
+                nc.scalar.activation(va[t][:, :V], va[t][:, V:], ACT.Tanh)
+            else:
+                nc.vector.tensor_tensor(va[t][:, :V], va[t][:, V::2], va[t][:, V + 1 :: 2], ALU.max)
 
         def look_up(t):
-            if t in SCALAR_VEN:
-                nc.scalar.activation(vv[t][:], va[t][:].indirect(ven_sb[:]), ACT.Copy)
-            else:
-                nc.vector.tensor_tensor(hv[t][:], va[t][:].indirect(ven_sb[:]), own_sb[t][:], ALU.add)
+            pieces = 2 if t in VECTOR_MAX else 1
+            width = S // pieces
+            for u in range(pieces):
+                cols = slice(width * u, width * (u + 1))
+                found = va[t][:].indirect(ven_sb[:, width // 16 * u : width // 16 * (u + 1)])
+                if t in SCALAR_VEN:
+                    nc.scalar.activation(vv[t][:, cols], found, ACT.Copy)
+                else:
+                    nc.vector.tensor_tensor(hv[t][:, cols], found, own_sb[t][:, cols], ALU.add)
 
         def add_own(t):
             if t in SCALAR_VEN:
@@ -153,19 +183,22 @@ def tile_picked_yhlgnn_silu_p_kernel(
             nc.scalar.activation(act[t][:], hv[t][:], ACT.Silu)
 
         def join(t, u):
+            a, b = PIECES[u]
             nc.vector.tensor_tensor(
                 g[t][u][:],
-                hv[t][:].indirect(coc_sb[:, 16 * u : 16 * (u + 1)]),
-                act[t][:, HALF * u : HALF * (u + 1)],
+                hv[t][:].indirect(coc_sb[:, a // 16 : b // 16]),
+                act[t][:, a:b],
                 ALU.add,
             )
 
-        hid_planes = [sb.tile([P, PACK, HALF], BF16, name=f"hid_planes{u}", align_bytes=64) for u in range(2)]
+        hid_planes = [
+            sb.tile([P, PACK, b - a], BF16, name=f"hid_planes{u}", align_bytes=64) for u, (a, b) in enumerate(PIECES)
+        ]
 
         def scale(t, u):
             nc.scalar.activation(hid_planes[u][:, t, :], g[t][u][:], ACT.Copy, scale=unit_sb[:, t : t + 1])
 
-        w_bf = sb.tile([P, N, PACK], BF16, name="w_bf", align_bytes=64)
+        w_bf = sb.tile([P, N, PACK], BF16, name="w_bf", tag="words1", align_bytes=64)
         w_codes = sb.tile([P, N], U32, name="w_codes", align_bytes=64)
         w_scales = sb.tile([P, N], U8, name="w_scales", align_bytes=64)
 
@@ -182,23 +215,26 @@ def tile_picked_yhlgnn_silu_p_kernel(
                 in_=w_bf[:].rearrange("p m j -> p (m j)"),
             )
 
-        hid_bf = [sb.tile([P, HALF, PACK], BF16, name=f"hid_bf{u}", align_bytes=64) for u in range(2)]
-        hid_codes = [sb.tile([P, HALF], U32, name=f"hid_codes{u}", align_bytes=64) for u in range(2)]
-        hid_scales = [sb.tile([P, HALF], U8, name=f"hid_scales{u}", align_bytes=64) for u in range(2)]
+        hid_bf = [sb.tile([P, b - a, PACK], BF16, name=f"hid_bf{u}", align_bytes=64) for u, (a, b) in enumerate(PIECES)]
+        hid_codes = [sb.tile([P, b - a], U32, name=f"hid_codes{u}", align_bytes=64) for u, (a, b) in enumerate(PIECES)]
+        hid_scales = [sb.tile([P, b - a], U8, name=f"hid_scales{u}", align_bytes=64) for u, (a, b) in enumerate(PIECES)]
 
         def interleave(u):
-            nc.vector.tensor_copy(
-                out=hid_bf[u][:].rearrange("p (c i) t -> p c t i", i=4),
-                in_=hid_planes[u][:].rearrange("p t (c i) -> p c t i", i=4),
-            )
+            dst = hid_bf[u][:].rearrange("p (c i) t -> p c t i", i=4)
+            src = hid_planes[u][:].rearrange("p t (c i) -> p c t i", i=4)
+            if u == LAST:
+                nc.scalar.copy(out=dst, in_=src)
+            else:
+                nc.vector.tensor_copy(out=dst, in_=src)
 
         def finish(u):
+            a, b = PIECES[u]
             nc.vector.quantize_mx(
                 out=hid_codes[u][:].bitcast(FP8X4),
                 scales=hid_scales[u][:],
                 in_=hid_bf[u][:].rearrange("p c t -> p (c t)"),
             )
-            acc = ps.tile([P, HALF], F32, name=f"acc{u}")
+            acc = ps.tile([P, b - a], F32, name=f"acc{u}")
             nc.tensor.matmul_mx(
                 out=acc[:],
                 lhsT=w_codes[:].bitcast(FP8X4),
@@ -208,47 +244,28 @@ def tile_picked_yhlgnn_silu_p_kernel(
                 start=True,
                 stop=True,
             )
-            res = sb.tile([P, HALF], F32, name=f"res{u}")
-            nc.scalar.copy(out=res[:], in_=acc[:])
-            nc.sync.dma_start(out=out[:, HALF * u : HALF * (u + 1)], in_=res[:])
+            res = sb.tile([P, b - a], F32, name=f"res{u}")
+            if u < LAST:
+                nc.scalar.copy(out=res[:], in_=acc[:])
+            else:
+                nc.vector.tensor_copy(out=res[:], in_=acc[:])
+            nc.sync.dma_start(out=out[:, a:b], in_=res[:])
 
-        bound(0)
-        pair_max(0)
-        bound(1)
-        pair_max(1)
-        look_up(0)
-        bound(2)
-        pair_max(2)
-        bound(3)
-        pair_max(3)
-        look_up(1)
-        silu(0)
-        look_up(2)
         round_w()
-        join(0, 0)
-        silu(1)
-        look_up(3)
         quantize_w()
-        add_own(2)
-        join(1, 0)
-        silu(2)
-        add_own(3)
-        join(0, 1)
-        silu(3)
-        join(2, 0)
-        scale(0, 0)
-        scale(1, 0)
-        join(3, 0)
-        scale(2, 0)
-        join(1, 1)
-        scale(3, 0)
-        join(2, 1)
-        scale(0, 1)
-        scale(1, 1)
-        join(3, 1)
-        scale(2, 1)
-        interleave(0)
-        scale(3, 1)
-        finish(0)
-        interleave(1)
-        finish(1)
+        for step in range(PACK + 2):
+            if step < PACK:
+                empty_bank(step)
+                venue(step)
+            if 1 <= step <= PACK:
+                look_up(step - 1)
+                add_own(step - 1)
+            if step >= 2:
+                silu(step - 2)
+        for u in range(len(PIECES)):
+            for t in range(PACK):
+                join(t, u)
+                scale(t, u)
+        for u in range(len(PIECES)):
+            interleave(u)
+            finish(u)

@@ -17,12 +17,20 @@ ALU = mybir.AluOpType
 
 P = 128
 PACK = 4
-PASSES = K // (P * PACK)
+K_PASS = P * PACK
+QUADRANT = 32
+SCALE_ROWS = 4
+LIST_ROWS = 16
 HALF = S // 2
-VECTOR_MAX = (1,)
+RUN = 4
+SPARE = 16
+
+EARLY_SCALE_LOADS = 5
+VECTOR_EMPTIES = 1
+VECTOR_LOOKS_UP = 0
 PIECES = ((0, 256), (256, 384), (384, 512))
-LAST = len(PIECES) - 1
-SCALAR_VEN = (1, 2, 3)
+LAST_PIECE = len(PIECES) - 1
+LAST_TILE = PACK - 1
 
 
 def tile_picked_yhlgnn_silu_p_kernel(
@@ -34,51 +42,48 @@ def tile_picked_yhlgnn_silu_p_kernel(
         sb = ctx.enter_context(tc.tile_pool(name="sb", bufs=1))
         ps = ctx.enter_context(tc.psum_pool(name="ps", bufs=1))
 
-        offs_sb = lists.tile([P, S // 16], U16, name="offs_sb")
-        ven_sb = lists.tile([P, S // 16], U16, name="ven_sb")
-        coc_sb = lists.tile([P, S // 16], U16, name="coc_sb")
+        offs_sb = lists.tile([P, S // LIST_ROWS], U16, name="offs_sb")
+        ven_sb = lists.tile([P, S // LIST_ROWS], U16, name="ven_sb")
+        coc_sb = lists.tile([P, S // LIST_ROWS], U16, name="coc_sb")
+
+        def entries(list_sb, a, b):
+            return list_sb[:, a // LIST_ROWS : b // LIST_ROWS]
 
         xs_all = sb.tile([P, T], U8, name="xs_all", align_bytes=64)
         nc.vector.memset(xs_all[:].bitcast(I32), 0)
-        for q in range(4):
-            nc.scalar.dma_start(
-                out=xs_all[32 * q : 32 * q + 8, :].bitcast(I32),
-                in_=x_scales[:, 4 * q : 4 * q + 4, :].bitcast(I32),
-            )
 
-        h_raw = [sb.tile([P, PACK, H], F32, name=f"h_raw{o}") for o in range(PASSES)]
-        xw_all = [sb.tile([P, T], I32, name=f"xw_all{o}", tag=f"words{o}", align_bytes=64) for o in range(PASSES)]
-        own_sb = [sb.tile([P, S], F32, name=f"own_sb{t}") for t in range(PACK)]
+        h_raw = [sb.tile([P, PACK, H], F32, name=f"h_raw{o}") for o in range(2)]
+        xw_all = [sb.tile([P, T], I32, name=f"xw_all{o}", tag=f"words{o}", align_bytes=64) for o in range(2)]
+        hv_own = [sb.tile([P, 2 * S], F32, name=f"hv_own{t}") for t in range(PACK)]
         unit_sb = sb.tile([P, PACK], F32, name="unit_sb")
         w_raw = sb.tile([P, PACK, N], F32, name="w_raw")
-
-        own_rows = own.rearrange("(p t) j -> p t j", t=PACK)
-
-        def load_x(o):
-            nc.sync.dma_start(
-                out=xw_all[o][:],
-                in_=x_words[o].rearrange("p n t -> p (n t)").bitcast(I32),
-            )
-
-        def load_w():
-            nc.sync.dma_start(out=w_raw[:], in_=w1.rearrange("(p j) m -> p j m", j=PACK))
-
-        def load_own(t):
-            nc.sync.dma_start(out=own_sb[t][:], in_=own_rows[:, t, :])
 
         def load_h(o):
             nc.sync.dma_start(
                 out=h_raw[o][:],
-                in_=hT[512 * o : 512 * (o + 1), :].rearrange("(p j) c -> p j c", j=PACK),
+                in_=hT[K_PASS * o : K_PASS * (o + 1), :].rearrange("(p j) c -> p j c", j=PACK),
             )
 
-        load_h(0)
-        load_h(1)
+        def load_scales(loads):
+            for o, r in loads:
+                nc.sync.dma_start(
+                    out=xs_all[SCALE_ROWS * o + r : P : QUADRANT, :].bitcast(I32),
+                    in_=x_scales[o, r::SCALE_ROWS, :].bitcast(I32),
+                )
+
+        def load_own(t):
+            nc.sync.dma_start(out=hv_own[t][:, S:], in_=own.rearrange("(p t) j -> p t j", t=PACK)[:, t, :])
+
+        scale_loads = [(o, r) for r in range(SCALE_ROWS) for o in range(2)]
         nc.sync.dma_start(offs_sb[:], offs)
+        load_h(0)
+        load_scales(scale_loads[:EARLY_SCALE_LOADS])
+        load_h(1)
+        load_scales(scale_loads[EARLY_SCALE_LOADS:])
+        for o in range(2):
+            nc.sync.dma_start(out=xw_all[o][:], in_=x_words[o].rearrange("p n t -> p (n t)").bitcast(I32))
         nc.sync.dma_start(ven_sb[:], ven)
-        load_x(0)
-        load_x(1)
-        load_w()
+        nc.sync.dma_start(out=w_raw[:], in_=w1.rearrange("(p j) m -> p j m", j=PACK))
         load_own(0)
         load_own(1)
         nc.sync.dma_start(coc_sb[:], coc)
@@ -91,181 +96,141 @@ def tile_picked_yhlgnn_silu_p_kernel(
         warm_out = sb.tile([P, 1], F32, name="warm_out")
         nc.scalar.activation(warm_out[:], warm[:], ACT.Silu)
 
-        h_codes = [sb.tile([P, H], U32, name=f"h_codes{o}", align_bytes=64) for o in range(PASSES)]
-        h_scales = [sb.tile([P, H], U8, name=f"h_scales{o}", align_bytes=64) for o in range(PASSES)]
-        h_bf = {}
-
-        def round_h(o, u):
-            h_bf[o, u] = sb.tile([P, 2, P, PACK], BF16, name=f"h_bf{o}{u}", align_bytes=64)
-            src = h_raw[o][:].rearrange("p j (m t) -> p m t j", t=PACK)[:, :, 2 * u : 2 * u + 2, :]
-            dst = h_bf[o, u][:].rearrange("p t m j -> p m t j")
-            if u == 0:
-                nc.vector.tensor_copy(out=dst, in_=src)
-            else:
-                nc.scalar.copy(out=dst, in_=src)
-
-        def quantize_h(o, u):
-            cols = slice(2 * P * u, 2 * P * (u + 1))
-            nc.vector.quantize_mx(
-                out=h_codes[o][:, cols].bitcast(FP8X4),
-                scales=h_scales[o][:, cols],
-                in_=h_bf[o, u][:].rearrange("p t m j -> p (t m j)"),
-            )
-
-        x_planes = sb.tile([P, S], U8, name="x_planes", align_bytes=64)
+        h_bf = [
+            [sb.tile([P, 2, P, PACK], BF16, name=f"h_bf{o}{pair}", align_bytes=64) for pair in range(2)]
+            for o in range(2)
+        ]
+        h_codes = [sb.tile([P, H], U32, name=f"h_codes{o}", align_bytes=64) for o in range(2)]
+        h_scales = [sb.tile([P, H], U8, name=f"h_scales{o}", align_bytes=64) for o in range(2)]
+        x_scale_bytes = sb.tile([P, S], U8, name="x_scale_bytes", align_bytes=64)
         y = [ps.tile([P, S], F32, name=f"y{t}") for t in range(PACK)]
 
-        def first_product(o, u):
-            half = slice(HALF * u, HALF * (u + 1))
-            x_codes = sb.tile([P, HALF], U32, name=f"x_codes{o}{u}", align_bytes=64)
-            nc.vector.tensor_copy(x_codes[:], xw_all[o][:].bitcast(U32).indirect(offs_sb[:, 16 * u : 16 * (u + 1)]))
-            for t in range(PACK):
-                cols = slice(P * t, P * (t + 1))
-                nc.tensor.matmul_mx(
-                    out=y[t][:, half],
-                    lhsT=h_codes[o][:, cols].bitcast(FP8X4),
-                    lhsT_scale=h_scales[o][:, cols],
-                    rhs=x_codes[:].bitcast(FP8X4),
-                    rhs_scale=x_planes[4 * o : P, half],
-                    start=(o == 0 and u == 0),
-                    stop=(o == PASSES - 1 and u == 1),
+        def round_h(o):
+            for pair, copy in enumerate((nc.vector.tensor_copy, nc.scalar.copy)):
+                copy(
+                    out=h_bf[o][pair][:].rearrange("p t m j -> p m t j"),
+                    in_=h_raw[o][:].rearrange("p j (m t) -> p m t j", t=PACK)[:, :, 2 * pair : 2 * pair + 2, :],
                 )
 
-        round_h(0, 0)
-        round_h(0, 1)
-        quantize_h(0, 0)
-        quantize_h(0, 1)
-        round_h(1, 0)
-        round_h(1, 1)
-        quantize_h(1, 0)
-        quantize_h(1, 1)
-        nc.vector.tensor_copy(x_planes[:], xs_all[:].indirect(offs_sb[:]))
-        for o in range(PASSES):
-            for u in range(2):
-                first_product(o, u)
-
-        va = [sb.tile([P, V + (V if t in VECTOR_MAX else S)], F32, name=f"va{t}") for t in range(PACK)]
-        hv = [sb.tile([P, S], F32, name=f"hv{t}") for t in range(PACK)]
-        vv = {t: sb.tile([P, S], F32, name=f"vv{t}") for t in SCALAR_VEN}
-        act = [sb.tile([P, S], F32, name=f"act{t}") for t in range(PACK)]
-        g = [[sb.tile([P, b - a], F32, name=f"g{t}{u}") for u, (a, b) in enumerate(PIECES)] for t in range(PACK)]
-
-        def empty_bank(t):
-            if t in VECTOR_MAX:
-                nc.vector.tensor_reduce(
-                    va[t][:, V:], y[t][:].rearrange("p (v d) -> p v d", d=2), mybir.AxisListType.X, ALU.max
+        def quantize_h(o):
+            for pair in range(2):
+                cols = slice(2 * P * pair, 2 * P * (pair + 1))
+                nc.vector.quantize_mx(
+                    out=h_codes[o][:, cols].bitcast(FP8X4),
+                    scales=h_scales[o][:, cols],
+                    in_=h_bf[o][pair][:].rearrange("p t m j -> p (t m j)"),
                 )
-            else:
-                nc.scalar.activation(va[t][:, V:], y[t][:], ACT.Tanh)
 
-        def venue(t):
-            if t in VECTOR_MAX:
-                nc.scalar.activation(va[t][:, :V], va[t][:, V:], ACT.Tanh)
-            else:
-                nc.vector.tensor_tensor(va[t][:, :V], va[t][:, V::2], va[t][:, V + 1 :: 2], ALU.max)
+        def first_product_pass(o):
+            x_codes = []
+            for side in range(2):
+                x_codes.append(sb.tile([P, HALF], U32, name=f"x_codes{o}{side}", align_bytes=64))
+                picked = entries(offs_sb, HALF * side, HALF * (side + 1))
+                nc.vector.tensor_copy(x_codes[side][:], xw_all[o][:].bitcast(U32).indirect(picked))
+            for pair in range(2):
+                for side in range(2):
+                    a, b = HALF * side, HALF * (side + 1)
+                    for t in (2 * pair, 2 * pair + 1):
+                        cols = slice(P * t, P * (t + 1))
+                        nc.tensor.matmul_mx(
+                            out=y[t][:, a:b],
+                            lhsT=h_codes[o][:, cols].bitcast(FP8X4),
+                            lhsT_scale=h_scales[o][:, cols],
+                            rhs=x_codes[side][:].bitcast(FP8X4),
+                            rhs_scale=x_scale_bytes[SCALE_ROWS * o : P, a:b],
+                            start=(o == 0 and side == 0),
+                            stop=(o == 1 and side == 1),
+                        )
 
-        def look_up(t):
-            pieces = 2 if t in VECTOR_MAX else 1
-            width = S // pieces
-            for u in range(pieces):
-                cols = slice(width * u, width * (u + 1))
-                found = va[t][:].indirect(ven_sb[:, width // 16 * u : width // 16 * (u + 1)])
-                if t in SCALAR_VEN:
-                    nc.scalar.activation(vv[t][:, cols], found, ACT.Copy)
-                else:
-                    nc.vector.tensor_tensor(hv[t][:, cols], found, own_sb[t][:, cols], ALU.add)
+        round_h(0)
+        quantize_h(0)
+        nc.vector.tensor_copy(x_scale_bytes[:], xs_all[:].indirect(offs_sb[:]))
+        round_h(1)
+        first_product_pass(0)
+        quantize_h(1)
+        first_product_pass(1)
 
-        def add_own(t):
-            if t in SCALAR_VEN:
-                nc.vector.tensor_tensor(hv[t][:], vv[t][:], own_sb[t][:], ALU.add)
-
-        def silu(t):
-            nc.scalar.activation(act[t][:], hv[t][:], ACT.Silu)
-
-        def join(t, u):
-            a, b = PIECES[u]
-            nc.vector.tensor_tensor(
-                g[t][u][:],
-                hv[t][:].indirect(coc_sb[:, a // 16 : b // 16]),
-                act[t][:, a:b],
-                ALU.add,
-            )
-
-        hid_planes = [
-            sb.tile([P, PACK, b - a], BF16, name=f"hid_planes{u}", align_bytes=64) for u, (a, b) in enumerate(PIECES)
-        ]
-
-        def scale(t, u):
-            nc.scalar.activation(hid_planes[u][:, t, :], g[t][u][:], ACT.Copy, scale=unit_sb[:, t : t + 1])
-
-        w_bf = sb.tile([P, N, PACK], BF16, name="w_bf", tag="words1", align_bytes=64)
-        w_codes = sb.tile([P, N], U32, name="w_codes", align_bytes=64)
+        w_bf = sb.tile([P, N, PACK], BF16, name="w_bf", tag="words0", align_bytes=64)
+        w_codes = sb.tile([P, N], U32, name="w_codes", tag="words1", align_bytes=64)
         w_scales = sb.tile([P, N], U8, name="w_scales", align_bytes=64)
+        nc.scalar.copy(
+            out=w_bf[:].rearrange("p (c i) j -> p c j i", i=RUN),
+            in_=w_raw[:].rearrange("p j (c i) -> p c j i", i=RUN),
+        )
+        nc.vector.quantize_mx(
+            out=w_codes[:].bitcast(FP8X4), scales=w_scales[:], in_=w_bf[:].rearrange("p m j -> p (m j)")
+        )
 
-        def round_w():
-            nc.vector.tensor_copy(
-                out=w_bf[:].rearrange("p (c i) j -> p c j i", i=4),
-                in_=w_raw[:].rearrange("p j (c i) -> p c j i", i=4),
-            )
+        venue = [
+            sb.tile([P, V + (V + SPARE if t == VECTOR_EMPTIES else S)], F32, name=f"venue{t}") for t in range(PACK)
+        ]
+        nc.vector.memset(venue[VECTOR_EMPTIES][:, 2 * V :], 0.0)
+        act = [sb.tile([P, S], F32, name=f"act{t}") for t in range(PACK)]
+        joined = [sb.tile([P, S], F32, name=f"joined{t}") for t in range(PACK)]
+        hid_rows = sb.tile([P, PACK, S], BF16, name="hid_rows", align_bytes=64)
 
-        def quantize_w():
-            nc.vector.quantize_mx(
-                out=w_codes[:].bitcast(FP8X4),
-                scales=w_scales[:],
-                in_=w_bf[:].rearrange("p m j -> p (m j)"),
-            )
-
-        hid_bf = [sb.tile([P, b - a, PACK], BF16, name=f"hid_bf{u}", align_bytes=64) for u, (a, b) in enumerate(PIECES)]
-        hid_codes = [sb.tile([P, b - a], U32, name=f"hid_codes{u}", align_bytes=64) for u, (a, b) in enumerate(PIECES)]
-        hid_scales = [sb.tile([P, b - a], U8, name=f"hid_scales{u}", align_bytes=64) for u, (a, b) in enumerate(PIECES)]
-
-        def interleave(u):
-            dst = hid_bf[u][:].rearrange("p (c i) t -> p c t i", i=4)
-            src = hid_planes[u][:].rearrange("p t (c i) -> p c t i", i=4)
-            if u == LAST:
-                nc.scalar.copy(out=dst, in_=src)
+        def make_venues(t):
+            if t == VECTOR_EMPTIES:
+                pairs = y[t][:].rearrange("p (v d) -> p v d", d=2)
+                nc.vector.tensor_reduce(venue[t][:, V : 2 * V], pairs, mybir.AxisListType.X, ALU.max)
+                nc.scalar.activation(venue[t][:, :V], venue[t][:, V : 2 * V], ACT.Tanh)
             else:
-                nc.vector.tensor_copy(out=dst, in_=src)
+                nc.scalar.activation(venue[t][:, V:], y[t][:], ACT.Tanh)
+                nc.vector.tensor_tensor(venue[t][:, :V], venue[t][:, V::2], venue[t][:, V + 1 :: 2], ALU.max)
 
-        def finish(u):
-            a, b = PIECES[u]
+        def make_hv(t):
+            vv = venue[t][:].indirect(ven_sb[:])
+            if t != VECTOR_LOOKS_UP:
+                vv_sb = sb.tile([P, S], F32, name=f"vv_sb{t}")
+                nc.scalar.activation(vv_sb[:], vv, ACT.Copy)
+                vv = vv_sb[:]
+            nc.vector.tensor_tensor(hv_own[t][:, :S], vv, hv_own[t][:, S:], ALU.add)
+
+        def column_ranges(t):
+            return PIECES if t == LAST_TILE else ((0, S),)
+
+        def join(t):
+            for a, b in column_ranges(t):
+                cited = hv_own[t][:].indirect(entries(coc_sb, a, b))
+                nc.vector.tensor_tensor(joined[t][:, a:b], cited, act[t][:, a:b], ALU.add)
+
+        for step in range(PACK + 3):
+            if step < PACK:
+                make_venues(step)
+            if 0 <= step - 1 < PACK:
+                make_hv(step - 1)
+            if 0 <= step - 2 < PACK:
+                nc.scalar.activation(act[step - 2][:], hv_own[step - 2][:, :S], ACT.Silu)
+            if 0 <= step - 3:
+                join(step - 3)
+
+        for t in range(PACK):
+            for a, b in column_ranges(t):
+                nc.scalar.activation(hid_rows[:, t, a:b], joined[t][:, a:b], ACT.Copy, scale=unit_sb[:, t : t + 1])
+
+        for u, (a, b) in enumerate(PIECES):
+            hid_bf = sb.tile([P, b - a, PACK], BF16, name=f"hid_bf{u}", align_bytes=64)
+            hid_codes = sb.tile([P, b - a], U32, name=f"hid_codes{u}", align_bytes=64)
+            hid_scales = sb.tile([P, b - a], U8, name=f"hid_scales{u}", align_bytes=64)
+            interleave = nc.scalar.copy if u == LAST_PIECE else nc.vector.tensor_copy
+            interleave(
+                out=hid_bf[:].rearrange("p (c i) t -> p c t i", i=RUN),
+                in_=hid_rows[:, :, a:b].rearrange("p t (c i) -> p c t i", i=RUN),
+            )
             nc.vector.quantize_mx(
-                out=hid_codes[u][:].bitcast(FP8X4),
-                scales=hid_scales[u][:],
-                in_=hid_bf[u][:].rearrange("p c t -> p (c t)"),
+                out=hid_codes[:].bitcast(FP8X4), scales=hid_scales[:], in_=hid_bf[:].rearrange("p c t -> p (c t)")
             )
             acc = ps.tile([P, b - a], F32, name=f"acc{u}")
             nc.tensor.matmul_mx(
                 out=acc[:],
                 lhsT=w_codes[:].bitcast(FP8X4),
                 lhsT_scale=w_scales[:],
-                rhs=hid_codes[u][:].bitcast(FP8X4),
-                rhs_scale=hid_scales[u][:],
+                rhs=hid_codes[:].bitcast(FP8X4),
+                rhs_scale=hid_scales[:],
                 start=True,
                 stop=True,
             )
             res = sb.tile([P, b - a], F32, name=f"res{u}")
-            if u < LAST:
-                nc.scalar.copy(out=res[:], in_=acc[:])
-            else:
-                nc.vector.tensor_copy(out=res[:], in_=acc[:])
+            empty_bank = nc.vector.tensor_copy if u == LAST_PIECE else nc.scalar.copy
+            empty_bank(out=res[:], in_=acc[:])
             nc.sync.dma_start(out=out[:, a:b], in_=res[:])
-
-        round_w()
-        quantize_w()
-        for step in range(PACK + 2):
-            if step < PACK:
-                empty_bank(step)
-                venue(step)
-            if 1 <= step <= PACK:
-                look_up(step - 1)
-                add_own(step - 1)
-            if step >= 2:
-                silu(step - 2)
-        for u in range(len(PIECES)):
-            for t in range(PACK):
-                join(t, u)
-                scale(t, u)
-        for u in range(len(PIECES)):
-            interleave(u)
-            finish(u)

from contextlib import ExitStack

import concourse.mybir as mybir

K, T, S, H, V, N = 1024, 2048, 512, 512, 256, 128
FLOPS = 2 * K * H * S + 2 * H * N * S

F32 = mybir.dt.float32
BF16 = mybir.dt.bfloat16
I32 = mybir.dt.int32
U32 = mybir.dt.uint32
U16 = mybir.dt.uint16
U8 = mybir.dt.uint8
FP8X4 = mybir.dt.float8_e4m3fn_x4
ACT = mybir.ActivationFunctionType
ALU = mybir.AluOpType

P = 128
PACK = 4
K_PASS = P * PACK
QUADRANT = 32
SCALE_ROWS = 4
LIST_ROWS = 16
HALF = S // 2
RUN = 4
SPARE = 16

EARLY_SCALE_LOADS = 5
VECTOR_EMPTIES = 1
VECTOR_LOOKS_UP = 0
PIECES = ((0, 256), (256, 384), (384, 512))
LAST_PIECE = len(PIECES) - 1
LAST_TILE = PACK - 1


def tile_picked_yhlgnn_silu_p_kernel(
    tc, x_words, x_scales, hT, own, unit, w1, offs, ven, coc, out
):
    nc = tc.nc
    with ExitStack() as ctx:
        lists = ctx.enter_context(tc.tile_pool(name="lists", bufs=1))
        sb = ctx.enter_context(tc.tile_pool(name="sb", bufs=1))
        ps = ctx.enter_context(tc.psum_pool(name="ps", bufs=1))

        offs_sb = lists.tile([P, S // LIST_ROWS], U16, name="offs_sb")
        ven_sb = lists.tile([P, S // LIST_ROWS], U16, name="ven_sb")
        coc_sb = lists.tile([P, S // LIST_ROWS], U16, name="coc_sb")

        def entries(list_sb, a, b):
            return list_sb[:, a // LIST_ROWS : b // LIST_ROWS]

        xs_all = sb.tile([P, T], U8, name="xs_all", align_bytes=64)
        nc.vector.memset(xs_all[:].bitcast(I32), 0)

        h_raw = [sb.tile([P, PACK, H], F32, name=f"h_raw{o}") for o in range(2)]
        xw_all = [sb.tile([P, T], I32, name=f"xw_all{o}", tag=f"words{o}", align_bytes=64) for o in range(2)]
        hv_own = [sb.tile([P, 2 * S], F32, name=f"hv_own{t}") for t in range(PACK)]
        unit_sb = sb.tile([P, PACK], F32, name="unit_sb")
        w_raw = sb.tile([P, PACK, N], F32, name="w_raw")

        def load_h(o):
            nc.sync.dma_start(
                out=h_raw[o][:],
                in_=hT[K_PASS * o : K_PASS * (o + 1), :].rearrange("(p j) c -> p j c", j=PACK),
            )

        def load_scales(loads):
            for o, r in loads:
                nc.sync.dma_start(
                    out=xs_all[SCALE_ROWS * o + r : P : QUADRANT, :].bitcast(I32),
                    in_=x_scales[o, r::SCALE_ROWS, :].bitcast(I32),
                )

        def load_own(t):
            nc.sync.dma_start(out=hv_own[t][:, S:], in_=own.rearrange("(p t) j -> p t j", t=PACK)[:, t, :])

        scale_loads = [(o, r) for r in range(SCALE_ROWS) for o in range(2)]
        nc.sync.dma_start(offs_sb[:], offs)
        load_h(0)
        load_scales(scale_loads[:EARLY_SCALE_LOADS])
        load_h(1)
        load_scales(scale_loads[EARLY_SCALE_LOADS:])
        for o in range(2):
            nc.sync.dma_start(out=xw_all[o][:], in_=x_words[o].rearrange("p n t -> p (n t)").bitcast(I32))
        nc.sync.dma_start(ven_sb[:], ven)
        nc.sync.dma_start(out=w_raw[:], in_=w1.rearrange("(p j) m -> p j m", j=PACK))
        load_own(0)
        load_own(1)
        nc.sync.dma_start(coc_sb[:], coc)
        load_own(2)
        load_own(3)
        nc.sync.dma_start(out=unit_sb[:], in_=unit.rearrange("(p t) o -> p (t o)", t=PACK))

        warm = sb.tile([P, 1], F32, name="warm")
        nc.vector.memset(warm[:], 0.0)
        warm_out = sb.tile([P, 1], F32, name="warm_out")
        nc.scalar.activation(warm_out[:], warm[:], ACT.Silu)

        h_bf = [
            [sb.tile([P, 2, P, PACK], BF16, name=f"h_bf{o}{pair}", align_bytes=64) for pair in range(2)]
            for o in range(2)
        ]
        h_codes = [sb.tile([P, H], U32, name=f"h_codes{o}", align_bytes=64) for o in range(2)]
        h_scales = [sb.tile([P, H], U8, name=f"h_scales{o}", align_bytes=64) for o in range(2)]
        x_scale_bytes = sb.tile([P, S], U8, name="x_scale_bytes", align_bytes=64)
        y = [ps.tile([P, S], F32, name=f"y{t}") for t in range(PACK)]

        def round_h(o):
            for pair, copy in enumerate((nc.vector.tensor_copy, nc.scalar.copy)):
                copy(
                    out=h_bf[o][pair][:].rearrange("p t m j -> p m t j"),
                    in_=h_raw[o][:].rearrange("p j (m t) -> p m t j", t=PACK)[:, :, 2 * pair : 2 * pair + 2, :],
                )

        def quantize_h(o):
            for pair in range(2):
                cols = slice(2 * P * pair, 2 * P * (pair + 1))
                nc.vector.quantize_mx(
                    out=h_codes[o][:, cols].bitcast(FP8X4),
                    scales=h_scales[o][:, cols],
                    in_=h_bf[o][pair][:].rearrange("p t m j -> p (t m j)"),
                )

        def first_product_pass(o):
            x_codes = []
            for side in range(2):
                x_codes.append(sb.tile([P, HALF], U32, name=f"x_codes{o}{side}", align_bytes=64))
                picked = entries(offs_sb, HALF * side, HALF * (side + 1))
                nc.vector.tensor_copy(x_codes[side][:], xw_all[o][:].bitcast(U32).indirect(picked))
            for pair in range(2):
                for side in range(2):
                    a, b = HALF * side, HALF * (side + 1)
                    for t in (2 * pair, 2 * pair + 1):
                        cols = slice(P * t, P * (t + 1))
                        nc.tensor.matmul_mx(
                            out=y[t][:, a:b],
                            lhsT=h_codes[o][:, cols].bitcast(FP8X4),
                            lhsT_scale=h_scales[o][:, cols],
                            rhs=x_codes[side][:].bitcast(FP8X4),
                            rhs_scale=x_scale_bytes[SCALE_ROWS * o : P, a:b],
                            start=(o == 0 and side == 0),
                            stop=(o == 1 and side == 1),
                        )

        round_h(0)
        quantize_h(0)
        nc.vector.tensor_copy(x_scale_bytes[:], xs_all[:].indirect(offs_sb[:]))
        round_h(1)
        first_product_pass(0)
        quantize_h(1)
        first_product_pass(1)

        w_bf = sb.tile([P, N, PACK], BF16, name="w_bf", tag="words0", align_bytes=64)
        w_codes = sb.tile([P, N], U32, name="w_codes", tag="words1", align_bytes=64)
        w_scales = sb.tile([P, N], U8, name="w_scales", align_bytes=64)
        nc.scalar.copy(
            out=w_bf[:].rearrange("p (c i) j -> p c j i", i=RUN),
            in_=w_raw[:].rearrange("p j (c i) -> p c j i", i=RUN),
        )
        nc.vector.quantize_mx(
            out=w_codes[:].bitcast(FP8X4), scales=w_scales[:], in_=w_bf[:].rearrange("p m j -> p (m j)")
        )

        venue = [
            sb.tile([P, V + (V + SPARE if t == VECTOR_EMPTIES else S)], F32, name=f"venue{t}") for t in range(PACK)
        ]
        nc.vector.memset(venue[VECTOR_EMPTIES][:, 2 * V :], 0.0)
        act = [sb.tile([P, S], F32, name=f"act{t}") for t in range(PACK)]
        joined = [sb.tile([P, S], F32, name=f"joined{t}") for t in range(PACK)]
        hid_rows = sb.tile([P, PACK, S], BF16, name="hid_rows", align_bytes=64)

        def make_venues(t):
            if t == VECTOR_EMPTIES:
                pairs = y[t][:].rearrange("p (v d) -> p v d", d=2)
                nc.vector.tensor_reduce(venue[t][:, V : 2 * V], pairs, mybir.AxisListType.X, ALU.max)
                nc.scalar.activation(venue[t][:, :V], venue[t][:, V : 2 * V], ACT.Tanh)
            else:
                nc.scalar.activation(venue[t][:, V:], y[t][:], ACT.Tanh)
                nc.vector.tensor_tensor(venue[t][:, :V], venue[t][:, V::2], venue[t][:, V + 1 :: 2], ALU.max)

        def make_hv(t):
            vv = venue[t][:].indirect(ven_sb[:])
            if t != VECTOR_LOOKS_UP:
                vv_sb = sb.tile([P, S], F32, name=f"vv_sb{t}")
                nc.scalar.activation(vv_sb[:], vv, ACT.Copy)
                vv = vv_sb[:]
            nc.vector.tensor_tensor(hv_own[t][:, :S], vv, hv_own[t][:, S:], ALU.add)

        def column_ranges(t):
            return PIECES if t == LAST_TILE else ((0, S),)

        def join(t):
            for a, b in column_ranges(t):
                cited = hv_own[t][:].indirect(entries(coc_sb, a, b))
                nc.vector.tensor_tensor(joined[t][:, a:b], cited, act[t][:, a:b], ALU.add)

        for step in range(PACK + 3):
            if step < PACK:
                make_venues(step)
            if 0 <= step - 1 < PACK:
                make_hv(step - 1)
            if 0 <= step - 2 < PACK:
                nc.scalar.activation(act[step - 2][:], hv_own[step - 2][:, :S], ACT.Silu)
            if 0 <= step - 3:
                join(step - 3)

        for t in range(PACK):
            for a, b in column_ranges(t):
                nc.scalar.activation(hid_rows[:, t, a:b], joined[t][:, a:b], ACT.Copy, scale=unit_sb[:, t : t + 1])

        for u, (a, b) in enumerate(PIECES):
            hid_bf = sb.tile([P, b - a, PACK], BF16, name=f"hid_bf{u}", align_bytes=64)
            hid_codes = sb.tile([P, b - a], U32, name=f"hid_codes{u}", align_bytes=64)
            hid_scales = sb.tile([P, b - a], U8, name=f"hid_scales{u}", align_bytes=64)
            interleave = nc.scalar.copy if u == LAST_PIECE else nc.vector.tensor_copy
            interleave(
                out=hid_bf[:].rearrange("p (c i) t -> p c t i", i=RUN),
                in_=hid_rows[:, :, a:b].rearrange("p t (c i) -> p c t i", i=RUN),
            )
            nc.vector.quantize_mx(
                out=hid_codes[:].bitcast(FP8X4), scales=hid_scales[:], in_=hid_bf[:].rearrange("p c t -> p (c t)")
            )
            acc = ps.tile([P, b - a], F32, name=f"acc{u}")
            nc.tensor.matmul_mx(
                out=acc[:],
                lhsT=w_codes[:].bitcast(FP8X4),
                lhsT_scale=w_scales[:],
                rhs=hid_codes[:].bitcast(FP8X4),
                rhs_scale=hid_scales[:],
                start=True,
                stop=True,
            )
            res = sb.tile([P, b - a], F32, name=f"res{u}")
            empty_bank = nc.vector.tensor_copy if u == LAST_PIECE else nc.scalar.copy
            empty_bank(out=res[:], in_=acc[:])
            nc.sync.dma_start(out=out[:, a:b], in_=res[:])
